import numpy as np, ml_dtypes
CORES = [78,86,94,102,110,118]
N = 6
def setup_inputs(rng):
    dy = rng.standard_normal((N, 128, N * 128), dtype=np.float32).astype(ml_dtypes.bfloat16)
    dyt = np.concatenate([dy[:, :, 128 * j:128 * j + 128].transpose(0, 2, 1) for j in range(N)], axis=2)
    return {"x": rng.standard_normal((N, 128, 128), dtype=np.float32).astype(ml_dtypes.bfloat16), "wt": rng.standard_normal((N, 128, 128), dtype=np.float32).astype(ml_dtypes.bfloat16), "dy": dy, "dyt": dyt}
def setup_inputs_big(rng):
    d = setup_inputs(rng)
    for k in ("x", "wt", "dy", "dyt"): d[k] = (d[k].astype(np.float32) * 1024.0).astype(d[k].dtype)
    return d
def setup_inputs_small(rng):
    d = setup_inputs(rng)
    for k in ("x", "wt", "dy", "dyt"): d[k] = (d[k].astype(np.float32) * (1 / 1024.0)).astype(d[k].dtype)
    return d
def setup_inputs_apart(rng):
    d = setup_inputs(rng)
    f = (10.0 ** rng.permutation(np.linspace(-1.5, 1.5, N))).astype(np.float32).reshape(N, 1, 1)
    for k in ("x", "wt", "dy", "dyt"): d[k] = (d[k].astype(np.float32) * f).astype(d[k].dtype)
    return d
def tie_inputs(x):
    x = dict(x)
    x["dyt"] = np.concatenate([x["dy"][:, :, 128 * j:128 * j + 128].transpose(0, 2, 1) for j in range(N)], axis=2)
    return x
def reference(x, wt, dy, dyt):
    X, WT, DY, DYT = x.astype(np.float64), wt.astype(np.float64), dy.astype(np.float64), dyt.astype(np.float64)
    dx = np.zeros((N, 128, 128)); dw = np.zeros((N, 128, 128))
    for r in range(N):
        for j in range(N):
            dx[r] += WT[j].T @ DY[j][:, 128 * r:128 * r + 128]
            dw[r] += X[j].T @ DYT[r][:, 128 * j:128 * j + 128]
    return {"dx": dx.astype(ml_dtypes.bfloat16 if x.dtype != np.float64 else np.float64), "dw": dw.astype(ml_dtypes.bfloat16 if x.dtype != np.float64 else np.float64)}

from concourse.bass import DstId, RemoteDMATransfer
from concourse.mybir import AluOpType

B = 128
N = 6

SCRATCH = {
    "wt_s": ("sbuf", [128, B], "bfloat16"),
    "dy_s": ("sbuf", [128, N * B], "bfloat16"),
    "dyt_s": ("sbuf", [128, N * B], "bfloat16"),
    "snd0": ("sbuf", [128, B], "bfloat16"),
    "snd1": ("sbuf", [128, 3 * B], "bfloat16"),
    "snd2": ("sbuf", [128, 3 * B], "bfloat16"),
    "lndx": ("sbuf", [128, B], "bfloat16"),
    "lnd0": ("sbuf", [128, B], "bfloat16"),
    "lnd1": ("sbuf", [128, 4 * B], "bfloat16"),
    "lnd2": ("sbuf", [128, 4 * B], "bfloat16"),
    "dx_s": ("sbuf", [128, B], "bfloat16"),
    "dw_s": ("sbuf", [128, B], "bfloat16"),
    "ps0": ("psum", [128, 512], "float32"),
    "ps1": ("psum", [128, 512], "float32"),
    "ps2": ("psum", [128, 512], "float32"),
    "acc": ("psum", [128, 512], "float32"),
    "psw": ("psum", [128, 512], "float32"),
}
SEMAPHORES = ["ld_x", "ld_wt", "ld_dy", "ld_dyt", "mm0", "mm1", "mm2", "mm3", "mmw", "cp0", "cp1", "cp2",
              "add", "dx_ok", "dw_ok", "st_dx", "st_dw", "sent", "in_x", "in_0", "in_1", "in_2"]


def _links(topo, a, b):
    ca, cb = topo.chip(a), topo.chip(b)
    if ca == cb:
        return 0
    return 1 if (topo.mates(ca, cb) or topo.same_plane(ca, cb)) else 2


def _offsets(topo, cores):
    n = len(cores)
    return sorted(range(1, n), key=lambda k: (-sum(_links(topo, cores[i], cores[(i + k) % n]) for i in range(n)), k))


def _bits(mask):
    return [b for b in range(mask.bit_length()) if (mask >> b) & 1]


def _mask(bits):
    return sum(1 << b for b in bits)


def rank_program(g, core, T, topo):
    r = T.rank_of(core)
    if r is None:
        return
    S = T.sem
    cores = list(T.cores)
    n = len(cores)
    k0, k1, k3, k2, k4 = _offsets(topo, cores)

    def to(k):
        return (r + k) % n

    def frm(k):
        return (r - k) % n

    def blk(j):
        return slice(B * j, B * j + B)

    for k in (k0, k1, k2, k3, k4):
        assert topo.may_write(core, cores[to(k)])

    g.sync.dma_start(T.snd1[:, B:2 * B], T.x[:, :]).then_inc(S.ld_x, 16)
    g.scalar.dma_start(T.dy_s[:, :], T.dy[:, :]).then_inc(S.ld_dy, 16)
    g.sync.dma_start(T.wt_s[:, :], T.wt[:, :]).then_inc(S.ld_wt, 16)
    g.scalar.dma_start(T.dyt_s[:, :], T.dyt[:, :]).then_inc(S.ld_dyt, 16)
    x_own = T.snd1[:, B:2 * B]

    te = g.tensor
    te.wait_ge(S.ld_wt, 16)
    te.wait_ge(S.ld_dy, 16)

    def partial(out, j, sem):
        te.matmul(out, T.wt_s[:, :], T.dy_s[:, blk(j)], start=True, stop=True).then_inc(sem, 1)

    partial(T.ps0[:, 0:B], to(k0), S.mm0)
    partial(T.ps1[:, 0:B], to(k1), S.mm1)
    partial(T.ps1[:, B:2 * B], to(k2), S.mm1)
    partial(T.ps2[:, 0:B], to(k3), S.mm2)
    partial(T.ps2[:, B:2 * B], to(k4), S.mm2)
    partial(T.acc[:, 0:B], r, S.mm3)

    def dw_term(x_ap, j, first=False, last=False):
        te.matmul(T.psw[:, 0:B], x_ap, T.dyt_s[:, blk(j)], start=first, stop=last).then_inc(S.mmw, 1)

    te.wait_ge(S.ld_x, 16)
    te.wait_ge(S.ld_dyt, 16)
    dw_term(x_own, r, first=True)
    te.wait_ge(S.in_x, 8)
    dw_term(T.lndx[:, :], frm(k0))
    te.wait_ge(S.in_1, 8)
    dw_term(T.lnd1[:, B:2 * B], frm(k1))
    dw_term(T.lnd1[:, 2 * B:3 * B], frm(k2))
    te.wait_ge(S.in_2, 8)
    dw_term(T.lnd2[:, B:2 * B], frm(k3))
    dw_term(T.lnd2[:, 2 * B:3 * B], frm(k4), last=True)

    ve = g.vector
    ve.wait_ge(S.ld_x, 16)
    ve.tensor_copy(T.snd2[:, B:2 * B], x_own).then_inc(S.cp2, 1)
    ve.wait_ge(S.mm0, 1)
    ve.tensor_copy(T.snd0[:, :], T.ps0[:, 0:B]).then_inc(S.cp0, 1)
    ve.wait_ge(S.mm1, 2)
    ve.tensor_copy(T.snd1[:, 0:B], T.ps1[:, 0:B]).then_inc(S.cp1, 1)
    ve.tensor_copy(T.snd1[:, 2 * B:3 * B], T.ps1[:, B:2 * B]).then_inc(S.cp1, 1)
    ve.wait_ge(S.mm2, 2)
    ve.tensor_copy(T.snd2[:, 0:B], T.ps2[:, 0:B]).then_inc(S.cp2, 1)
    ve.tensor_copy(T.snd2[:, 2 * B:3 * B], T.ps2[:, B:2 * B]).then_inc(S.cp2, 1)

    def slot(i):
        return T.acc[:, blk(i % 4)]

    ve.wait_ge(S.mm3, 1)
    ve.wait_ge(S.in_0, 8)
    ve.tensor_tensor(slot(1), slot(0), T.lnd0[:, :], AluOpType.add).then_inc(S.add, 1)
    ve.wait_ge(S.in_1, 8)
    ve.wait_ge(S.add, 1)
    ve.tensor_tensor(slot(2), slot(1), T.lnd1[:, 0:B], AluOpType.add).then_inc(S.add, 1)
    ve.wait_ge(S.add, 2)
    ve.tensor_tensor(slot(3), slot(2), T.lnd1[:, 3 * B:4 * B], AluOpType.add).then_inc(S.add, 1)
    ve.wait_ge(S.in_2, 8)
    ve.wait_ge(S.add, 3)
    ve.tensor_tensor(slot(4), slot(3), T.lnd2[:, 0:B], AluOpType.add).then_inc(S.add, 1)
    ve.wait_ge(S.add, 4)
    ve.tensor_tensor(T.dx_s[:, :], slot(4), T.lnd2[:, 3 * B:4 * B], AluOpType.add).then_inc(S.dx_ok, 1)
    ve.wait_ge(S.mmw, 6)
    ve.tensor_copy(T.dw_s[:, :], T.psw[:, 0:B]).then_inc(S.dw_ok, 1)

    def whole(dst_rank, out_ap, in_ap, sem):
        dst = cores[dst_rank]
        rid, pid, _ = topo.addr(dst)
        g.remote_dma(out_ap=out_ap, in_ap=in_ap, remote_sem=sem, local_sem=S.sent, pid=pid, routing_id=rid,
                     dma_engine_mask=topo.mask(core, dst))

    def pair(ka, kb, snd, lnd, sem):
        da, db = cores[to(ka)], cores[to(kb)]
        bits = _bits(topo.mask(core, da) & topo.mask(core, db))
        half = len(bits) // 2
        ra, pa, _ = topo.addr(da)
        rb, pb, _ = topo.addr(db)
        g.remote_dma_fused([
            RemoteDMATransfer(dst_ids=[DstId(rid=ra, pnc=pa)], dma_engine_mask=_mask(bits[:half]), remote_sem=sem,
                              src=snd[:, 0:2 * B], dst=lnd[:, 0:2 * B]),
            RemoteDMATransfer(dst_ids=[DstId(rid=rb, pnc=pb)], dma_engine_mask=_mask(bits[half:]), remote_sem=sem,
                              src=snd[:, B:3 * B], dst=lnd[:, 2 * B:4 * B]),
        ], local_sem=S.sent)

    g.wait_ge(S.ld_x, 16)
    whole(to(k0), T.lndx[:, :], x_own, S.in_x)
    g.wait_ge(S.cp0, 1)
    whole(to(k0), T.lnd0[:, :], T.snd0[:, :], S.in_0)
    g.wait_ge(S.cp1, 2)
    pair(k1, k2, T.snd1, T.lnd1, S.in_1)
    g.wait_ge(S.cp2, 3)
    pair(k3, k4, T.snd2, T.lnd2, S.in_2)
    g.wait_ge(S.sent, 32)

    g.sync.wait_ge(S.dx_ok, 1)
    g.sync.dma_start(T.dx[:, :], T.dx_s[:, :]).then_inc(S.st_dx, 16)
    g.sync.wait_ge(S.st_dx, 16)
    g.scalar.wait_ge(S.dw_ok, 1)
    g.scalar.dma_start(T.dw[:, :], T.dw_s[:, :]).then_inc(S.st_dw, 16)
    g.scalar.wait_ge(S.st_dw, 16)
